import numpy as np
import ml_dtypes


def mxq(x, axis, fmt="e4m3"):
    dtype, down = {"e4m3": (ml_dtypes.float8_e4m3fn, 7), "e5m2": (ml_dtypes.float8_e5m2, 14)}[fmt]
    v = np.moveaxis(np.asarray(x, np.float32).astype(ml_dtypes.bfloat16).astype(np.float64), axis, -1)
    blocks = v.reshape(v.shape[:-1] + (-1, 32))
    amax = np.abs(blocks).max(-1, keepdims=True)
    byte = np.maximum(np.where(amax > 0, np.frexp(amax)[1] - 1 + 127, 0) - down, 1)
    scale = np.exp2(byte - 127.0)
    codes = (blocks / scale).astype(np.float32).astype(dtype).astype(np.float64)
    return np.moveaxis((codes * scale).reshape(v.shape), -1, axis)


WIDE = False


def mx_kscale(k):
    if not WIDE:
        return np.ones(k)
    levels = np.array([10, -10, 5, -5, 0])
    if k % 512:
        return np.exp2(np.random.permutation(np.resize(levels, k // 32))).repeat(32)
    a = np.empty((k // 512, 16))
    for p in range(k // 512):
        a[p, :8] = np.random.permutation(np.resize(levels, 8))
        for g in range(8):
            far = levels[np.abs(levels - a[p, g]) >= 10]
            a[p, g + 8] = far[np.random.randint(len(far))]
    return np.exp2(a.ravel()).repeat(32)


BF16 = ml_dtypes.bfloat16


def bf(x):
    return np.asarray(x, np.float32).astype(BF16)


def f64(x):
    return np.asarray(x).astype(np.float64)


M, K, N, R = 2048, 1024, 1024, 512


def setup_inputs():
    s = mx_kscale(K)
    t = mx_kscale(M)
    a = np.random.standard_normal((M, K)) * s
    b = np.random.standard_normal((K, N)) / np.sqrt(K) / s[:, None]
    w = (1 + 0.1 * np.random.standard_normal(M)) * t
    enc = np.random.standard_normal((R, M)) / np.sqrt(M) / t
    parity = np.random.standard_normal((R, K)) * s
    tol = 0.5 + 0.1 * np.abs(np.random.standard_normal(N))
    return {"a": bf(a), "b": bf(b), "w": bf(w), "enc": bf(enc), "parity": bf(parity), "tol": bf(tol)}


def reference(a, b, w, enc, parity, tol):
    bq = mxq(f64(b), 0, "e4m3")
    c = mxq(f64(a), 1, "e4m3") @ bq
    cw = c * f64(w)[:, None]
    seen = mxq(f64(enc), 1, "e4m3") @ mxq(cw, 0, "e4m3")
    told = mxq(f64(parity), 1, "e4m3") @ bq
    d = seen + told
    alarm = np.maximum(np.abs(d), f64(tol))
    return c, alarm

@@ -1,0 +1,249 @@
+from contextlib import ExitStack
+
+import concourse.mybir as mybir
+from concourse.masks import make_identity
+
+M, K, N, R = 2048, 1024, 1024, 512
+FLOPS = 2 * M * K * N + 2 * R * M * N + 2 * R * K * N
+
+F32 = mybir.dt.float32
+BF16 = mybir.dt.bfloat16
+U32 = mybir.dt.uint32
+U8 = mybir.dt.uint8
+FP8X4 = mybir.dt.float8_e4m3fn_x4
+ALU = mybir.AluOpType
+ACT = mybir.ActivationFunctionType
+
+P = 128
+PACK = 4
+SPAN = P * PACK
+HALF = 512
+CHUNK = 128
+BANKS = 8
+K_PASSES = K // SPAN
+M_GROUPS = M // SPAN
+R_TILES = R // P
+
+
+def tile_checksum_verified_product_s7_kernel(tc, a, b, w, enc, parity, tol, out_0, out_1):
+    nc = tc.nc
+    with ExitStack() as ctx:
+        keep = ctx.enter_context(tc.tile_pool(name="keep", bufs=1))
+        stage = ctx.enter_context(tc.tile_pool(name="stage", bufs=3))
+        psum = ctx.enter_context(tc.psum_pool(name="psum", bufs=1))
+        ctx.enter_context(tc.manual_schedule())
+
+        taken = []
+
+        def new_bank():
+            name = "bank%d" % (len(taken) % BANKS)
+            taken.append(name)
+            return psum.tile([P, HALF], F32, name=name)
+
+        def load(name, shape, source, engine):
+            t = keep.tile(shape, BF16, name=name, align_bytes=64)
+            engine.dma_start(out=t[:], in_=source)
+            return t
+
+        def operand(name):
+            codes = keep.tile([P, HALF], U32, name=name + "_codes", align_bytes=64)
+            scales = keep.tile([P, HALF], U8, name=name + "_scales", align_bytes=64)
+            return codes, scales
+
+        def quantize(name, grouped):
+            codes, scales = operand(name)
+            nc.vector.quantize_mx(out=codes[:].bitcast(FP8X4), scales=scales[:], in_=grouped[:])
+            return codes, scales
+
+        def mx(out, lhs, lhs_at, rhs, rhs_at, width, start, stop):
+            lc = slice(lhs_at, lhs_at + P)
+            rc = slice(rhs_at, rhs_at + width)
+            nc.tensor.matmul_mx(
+                out=out,
+                lhsT=lhs[0][:, lc].bitcast(FP8X4), lhsT_scale=lhs[1][:, lc],
+                rhs=rhs[0][:, rc].bitcast(FP8X4), rhs_scale=rhs[1][:, rc],
+                start=start, stop=stop,
+            )
+
+        a_rows = a.rearrange("(g p t) k -> g p t k", p=P, t=PACK)
+        b_rows = b.rearrange("(c p j) n -> c p j n", p=P, j=PACK)
+        w_sb = load("w_sb", [P, M_GROUPS, PACK], w.rearrange("(g p t) -> p g t", p=P, t=PACK), nc.scalar)
+        tol_cols = load("tol_cols", [P, N // P], tol.rearrange("(p x) -> p x", p=P), nc.scalar)
+
+        a_src = {}
+        b_raw = {}
+
+        def load_b(h, c):
+            b_raw[h, c] = load("b_raw%d%d" % (h, c), [P, PACK, HALF], b_rows[c][:, :, h * HALF:(h + 1) * HALF], nc.sync)
+
+        for c in range(K_PASSES):
+            t0 = load("a_raw0%d" % c, [P, PACK, SPAN], a_rows[0][:, :, c * SPAN:(c + 1) * SPAN], nc.sync)
+            a_src[0, c] = [t0[:, t, :] for t in range(PACK)]
+            load_b(0, c)
+        for g in range(1, M_GROUPS):
+            tg = load("a_raw%d" % g, [P, PACK, K], a_rows[g], nc.sync)
+            for c in range(K_PASSES):
+                a_src[g, c] = [tg[:, t, c * SPAN:(c + 1) * SPAN] for t in range(PACK)]
+        for c in range(K_PASSES):
+            load_b(1, c)
+        enc_src = {}
+        par_src = {}
+        par_rows = parity.rearrange("(q j p) k -> q p j k", p=P, j=2)
+        for j in range(R_TILES):
+            te = load("enc_raw%d" % j, [P, M], enc[j * P:(j + 1) * P, :], nc.sync)
+            enc_src[j] = [te[:, g * SPAN:(g + 1) * SPAN] for g in range(M_GROUPS)]
+            if j % 2 == 0:
+                tp = load("par_raw%d" % (j // 2), [P, 2, K], par_rows[j // 2], nc.sync)
+                par_src[j // 2] = [tp[:, x, c * SPAN:(c + 1) * SPAN] for x in range(2) for c in range(K_PASSES)]
+
+        ident = keep.tile([P, P], F32, name="ident")
+        make_identity(nc, ident[:])
+        ident_abs = keep.tile([P, P], F32, name="ident_abs")
+        nc.scalar.activation(out=ident_abs[:], in_=ident[:], func=ACT.Abs)
+
+        def turn(sources):
+            grouped = stage.tile([P, PACK * SPAN], BF16, name="turned", align_bytes=64)
+            words_out = grouped[:].bitcast(F32)
+            for pair in range(2):
+                bank = new_bank()
+                for x in range(2):
+                    words = sources[2 * pair + x].bitcast(F32)
+                    for u in range(2):
+                        at = (2 * x + u) * P
+                        nc.tensor.transpose(bank[:, at:at + P], words[:, u:2 * P:2], ident[:])
+                nc.scalar.copy(
+                    out=words_out[:, pair * HALF:(pair + 1) * HALF].rearrange("p (x r u) -> p x r u", x=2, u=2),
+                    in_=bank[:].rearrange("p (x u r) -> p x r u", x=2, u=2),
+                )
+            return grouped
+
+        def interleave(raw):
+            grouped = stage.tile([P, PACK * HALF], BF16, name="b_grouped", align_bytes=64, bufs=2)
+            nc.vector.tensor_copy(
+                out=grouped[:].rearrange("p (c i t) -> p c t i", i=4, t=PACK),
+                in_=raw[:].rearrange("p t (c i) -> p c t i", i=4),
+            )
+            return grouped
+
+        a_q = {}
+        b_q = {}
+        enc_q = {}
+        par_q = {}
+        cw_q = {}
+        c_rows = out_0.rearrange("(g p t) n -> g p t n", p=P, t=PACK)
+
+        def new_c_tiles():
+            c_sb = stage.tile([P, PACK, HALF], F32, name="c_sb", bufs=5)
+            cw = stage.tile([P, PACK * HALF], BF16, name="cw", align_bytes=64, bufs=2)
+            return c_sb, cw
+
+        def product(g, h, chunk, tiles):
+            c_sb, cw = tiles
+            bank = new_bank()
+            for t in range(PACK):
+                for c in range(K_PASSES):
+                    mx(bank[:, t * CHUNK:(t + 1) * CHUNK], a_q[g, c], t * P, b_q[h, c], chunk * CHUNK, CHUNK,
+                       c == 0, c == K_PASSES - 1)
+            nc.vector.tensor_tensor(
+                out=cw[:, chunk * HALF:(chunk + 1) * HALF].rearrange("p (n t) -> p n t", t=PACK),
+                in0=bank[:].rearrange("p (t n) -> p n t", t=PACK),
+                in1=w_sb[:, g:g + 1, :].to_broadcast([P, CHUNK, PACK]),
+                op=ALU.mult,
+            )
+            nc.scalar.copy(out=c_sb[:, :, chunk * CHUNK:(chunk + 1) * CHUNK],
+                           in_=bank[:].rearrange("p (t n) -> p t n", t=PACK))
+            if chunk == HALF // CHUNK - 1:
+                nc.sync.dma_start(out=c_rows[g][:, :, h * HALF:(h + 1) * HALF], in_=c_sb[:])
+
+        tol_sb = keep.tile([P, N], BF16, name="tol_sb", align_bytes=64)
+
+        def spread_tol():
+            bank = new_bank()
+            words = tol_cols[:].bitcast(F32)
+            for x in range(4):
+                nc.tensor.transpose(bank[:, x * P:(x + 1) * P], words[:, x:x + 1].to_broadcast([P, P]), ident_abs[:])
+            nc.scalar.copy(out=tol_sb[:].bitcast(F32).rearrange("p (r x) -> p r x", x=4),
+                           in_=bank[:].rearrange("p (x r) -> p r x", x=4))
+
+        def check_matmuls(h, j):
+            bank = new_bank()
+            for c in range(K_PASSES):
+                mx(bank[:], par_q[j // 2], ((j % 2) * K_PASSES + c) * P, b_q[h, c], 0, HALF, c == 0, False)
+            for g in range(M_GROUPS):
+                mx(bank[:], enc_q[j], g * P, cw_q[g, h], 0, HALF, False, g == M_GROUPS - 1)
+            size = stage.tile([P, HALF], F32, name="size")
+            nc.scalar.activation(out=size[:], in_=bank[:], func=ACT.Abs)
+            return size
+
+        def check_finish(h, j, size):
+            alarm = stage.tile([P, HALF], F32, name="alarm")
+            nc.vector.tensor_tensor(out=alarm[:], in0=size[:], in1=tol_sb[:, h * HALF:(h + 1) * HALF], op=ALU.max)
+            nc.sync.dma_start(out=out_1[j * P:(j + 1) * P, h * HALF:(h + 1) * HALF], in_=alarm[:])
+
+        ta0 = turn(a_src[0, 0])
+        gb0 = interleave(b_raw[0, 0])
+        a_q[0, 0] = quantize("a00", ta0)
+        b_q[0, 0] = quantize("b00", gb0)
+        ta1 = turn(a_src[0, 1])
+        gb1 = interleave(b_raw[0, 1])
+        a_q[0, 1] = quantize("a01", ta1)
+        b_q[0, 1] = quantize("b01", gb1)
+        spread_tol()
+
+        def step(g, h, pair, pending, extra, early=0):
+            tiles = new_c_tiles()
+            for chunk in range(early):
+                product(g, h, chunk, tiles)
+            turned = [turn(x[3]) for x in pair]
+            for job in pending + extra:
+                job()
+            chunk = early
+            for x, grouped in zip(pair, turned):
+                x[0][x[1]] = quantize(x[2], grouped)
+                product(g, h, chunk, tiles)
+                chunk = chunk + 1
+            for rest in range(chunk, HALF // CHUNK):
+                product(g, h, rest, tiles)
+
+            def finish():
+                cw_q[g, h] = quantize("cw%d%d" % (g, h), tiles[1])
+            return [finish]
+
+        def a_pair(g):
+            return [(a_q, (g, c), "a%d%d" % (g, c), a_src[g, c]) for c in range(K_PASSES)]
+
+        def enc_unit(j):
+            return (enc_q, j, "enc%d" % j, enc_src[j])
+
+        def par_unit(q):
+            return (par_q, q, "par%d" % q, par_src[q])
+
+        b_late = {}
+
+        def b_interleave(c):
+            def job():
+                b_late[c] = interleave(b_raw[1, c])
+            return job
+
+        def b_quantize(c):
+            def job():
+                b_q[1, c] = quantize("b1%d" % c, b_late[c])
+            return job
+
+        pending = step(0, 0, a_pair(1), [], [], early=2)
+        pending = step(1, 0, a_pair(2), pending, [b_interleave(0)])
+        pending = step(2, 0, a_pair(3), pending, [b_quantize(0), b_interleave(1)])
+        pending = step(3, 0, [enc_unit(0), par_unit(0)], pending, [b_quantize(1)])
+        pending = step(0, 1, [enc_unit(1), enc_unit(2)], pending, [])
+        size = check_matmuls(0, 0)
+        pending = step(1, 1, [], pending, [lambda: check_finish(0, 0, size)])
+        pending = step(2, 1, [enc_unit(3), par_unit(1)], pending, [])
+        size1 = check_matmuls(0, 1)
+        pending = step(3, 1, [], pending, [lambda: check_finish(0, 1, size1)])
+        rest = [(0, 2), (0, 3), (1, 0), (1, 1), (1, 2), (1, 3)]
+        for h, j in rest:
+            size2 = check_matmuls(h, j)
+            for job in pending:
+                job()
+            pending = []
+            check_finish(h, j, size2)

@@ -18,11 +18,26 @@ P = 128
 PACK = 4
 SPAN = P * PACK
 HALF = 512
+QUARTER = 256
 CHUNK = 128
 BANKS = 8
 K_PASSES = K // SPAN
 M_GROUPS = M // SPAN
 R_TILES = R // P
+RANGES = (4, 2, 2)
+TURN_AFTER = [0, 1, 2, 4, 6, 8, 10, 12, 14, 16, 18, 20]
+SORT_BY = "nvnvnvnvnvnv"
+SORT_LEAD = 3
+TQ_LAG = 1
+CWQ_LAG = 1
+CHECK_AFTER = [19, 21, 23, 25, 27, 29]
+B_AFTER = [-1, -1, 6, 10, 18, 20]
+B_BY = "vvvvvv"
+B_LAG = 1
+S_FIRST = True
+C_LAG = 0
+MAX_LAG = 2
+WARM = [4, 4, 3]
 
 
 def tile_checksum_verified_product_s7_kernel(tc, a, b, w, enc, parity, tol, out_0, out_1):
@@ -45,13 +60,13 @@ def tile_checksum_verified_product_s7_kernel(tc, a, b, w, enc, parity, tol, out_
             engine.dma_start(out=t[:], in_=source)
             return t
 
-        def operand(name):
-            codes = keep.tile([P, HALF], U32, name=name + "_codes", align_bytes=64)
-            scales = keep.tile([P, HALF], U8, name=name + "_scales", align_bytes=64)
+        def operand(name, width=HALF):
+            codes = keep.tile([P, width], U32, name=name + "_codes", align_bytes=64)
+            scales = keep.tile([P, width], U8, name=name + "_scales", align_bytes=64)
             return codes, scales
 
         def quantize(name, grouped):
-            codes, scales = operand(name)
+            codes, scales = operand(name, grouped.shape[1] // PACK)
             nc.vector.quantize_mx(out=codes[:].bitcast(FP8X4), scales=scales[:], in_=grouped[:])
             return codes, scales
 
@@ -78,12 +93,12 @@ def tile_checksum_verified_product_s7_kernel(tc, a, b, w, enc, parity, tol, out_
 
         for c in range(K_PASSES):
             t0 = load("a_raw0%d" % c, [P, PACK, SPAN], a_rows[0][:, :, c * SPAN:(c + 1) * SPAN], nc.sync)
-            a_src[0, c] = [t0[:, t, :] for t in range(PACK)]
+            a_src[0, c] = t0[:]
             load_b(0, c)
         for g in range(1, M_GROUPS):
             tg = load("a_raw%d" % g, [P, PACK, K], a_rows[g], nc.sync)
             for c in range(K_PASSES):
-                a_src[g, c] = [tg[:, t, c * SPAN:(c + 1) * SPAN] for t in range(PACK)]
+                a_src[g, c] = tg[:, :, c * SPAN:(c + 1) * SPAN]
         for c in range(K_PASSES):
             load_b(1, c)
         enc_src = {}
@@ -91,69 +106,86 @@ def tile_checksum_verified_product_s7_kernel(tc, a, b, w, enc, parity, tol, out_
         par_rows = parity.rearrange("(q j p) k -> q p j k", p=P, j=2)
         for j in range(R_TILES):
             te = load("enc_raw%d" % j, [P, M], enc[j * P:(j + 1) * P, :], nc.sync)
-            enc_src[j] = [te[:, g * SPAN:(g + 1) * SPAN] for g in range(M_GROUPS)]
+            enc_src[j] = te[:].rearrange("p (g k) -> p g k", k=SPAN)
             if j % 2 == 0:
                 tp = load("par_raw%d" % (j // 2), [P, 2, K], par_rows[j // 2], nc.sync)
-                par_src[j // 2] = [tp[:, x, c * SPAN:(c + 1) * SPAN] for x in range(2) for c in range(K_PASSES)]
+                par_src[j // 2] = tp[:].rearrange("p x (c k) -> p (x c) k", k=SPAN)
 
         ident = keep.tile([P, P], F32, name="ident")
         make_identity(nc, ident[:])
         ident_abs = keep.tile([P, P], F32, name="ident_abs")
         nc.scalar.activation(out=ident_abs[:], in_=ident[:], func=ACT.Abs)
 
-        def turn(sources):
+        def sort_words(source, copy):
+            ordered = stage.tile([P, PACK, 2, P], F32, name="ordered", bufs=3)
+            copy(out=ordered[:], in_=source.bitcast(F32).rearrange("p s (x u) -> p s u x", u=2))
+            return [[ordered[:, s, u, :] for u in range(2)] for s in range(PACK)]
+
+        def stepped_words(source):
+            words = source.bitcast(F32)
+            return [[words[:, s, u:2 * P:2] for u in range(2)] for s in range(PACK)]
+
+        def turn(words):
             grouped = stage.tile([P, PACK * SPAN], BF16, name="turned", align_bytes=64)
             words_out = grouped[:].bitcast(F32)
             for pair in range(2):
                 bank = new_bank()
                 for x in range(2):
-                    words = sources[2 * pair + x].bitcast(F32)
                     for u in range(2):
                         at = (2 * x + u) * P
-                        nc.tensor.transpose(bank[:, at:at + P], words[:, u:2 * P:2], ident[:])
+                        nc.tensor.transpose(bank[:, at:at + P], words[2 * pair + x][u], ident[:])
                 nc.scalar.copy(
                     out=words_out[:, pair * HALF:(pair + 1) * HALF].rearrange("p (x r u) -> p x r u", x=2, u=2),
                     in_=bank[:].rearrange("p (x u r) -> p x r u", x=2, u=2),
                 )
             return grouped
 
-        def interleave(raw):
-            grouped = stage.tile([P, PACK * HALF], BF16, name="b_grouped", align_bytes=64, bufs=2)
-            nc.vector.tensor_copy(
+        def interleave(h, c, q, copy):
+            grouped = stage.tile([P, PACK * QUARTER], BF16, name="b_grouped", align_bytes=64, bufs=4)
+            copy(
                 out=grouped[:].rearrange("p (c i t) -> p c t i", i=4, t=PACK),
-                in_=raw[:].rearrange("p t (c i) -> p c t i", i=4),
+                in_=b_raw[h, c][:, :, q * QUARTER:(q + 1) * QUARTER].rearrange("p t (c i) -> p c t i", i=4),
             )
             return grouped
 
+        def quantize_b(h, c, q, grouped):
+            codes, scales = b_q[c]
+            cols = slice((2 * h + q) * QUARTER, (2 * h + q + 1) * QUARTER)
+            nc.vector.quantize_mx(out=codes[:, cols].bitcast(FP8X4), scales=scales[:, cols], in_=grouped[:])
+
         a_q = {}
-        b_q = {}
+        b_q = {c: operand("b%d" % c, N) for c in range(K_PASSES)}
         enc_q = {}
         par_q = {}
         cw_q = {}
         c_rows = out_0.rearrange("(g p t) n -> g p t n", p=P, t=PACK)
 
-        def new_c_tiles():
-            c_sb = stage.tile([P, PACK, HALF], F32, name="c_sb", bufs=5)
-            cw = stage.tile([P, PACK * HALF], BF16, name="cw", align_bytes=64, bufs=2)
+        def new_c_tiles(chunks):
+            c_sb = stage.tile([P, PACK, chunks * CHUNK], F32, name="c_sb", bufs=4)
+            cw = stage.tile([P, PACK * chunks * CHUNK], BF16, name="cw", align_bytes=64, bufs=2)
             return c_sb, cw
 
-        def product(g, h, chunk, tiles):
-            c_sb, cw = tiles
+        def product(g, col):
             bank = new_bank()
             for t in range(PACK):
                 for c in range(K_PASSES):
-                    mx(bank[:, t * CHUNK:(t + 1) * CHUNK], a_q[g, c], t * P, b_q[h, c], chunk * CHUNK, CHUNK,
+                    mx(bank[:, t * CHUNK:(t + 1) * CHUNK], a_q[g, c], t * P, b_q[c], col, CHUNK,
                        c == 0, c == K_PASSES - 1)
+            return bank
+
+        def weigh(g, chunk, bank, cw):
             nc.vector.tensor_tensor(
                 out=cw[:, chunk * HALF:(chunk + 1) * HALF].rearrange("p (n t) -> p n t", t=PACK),
                 in0=bank[:].rearrange("p (t n) -> p n t", t=PACK),
                 in1=w_sb[:, g:g + 1, :].to_broadcast([P, CHUNK, PACK]),
                 op=ALU.mult,
             )
+
+        def keep_c(g, first, chunk, chunks, bank, c_sb):
             nc.scalar.copy(out=c_sb[:, :, chunk * CHUNK:(chunk + 1) * CHUNK],
                            in_=bank[:].rearrange("p (t n) -> p t n", t=PACK))
-            if chunk == HALF // CHUNK - 1:
-                nc.sync.dma_start(out=c_rows[g][:, :, h * HALF:(h + 1) * HALF], in_=c_sb[:])
+            if chunk == chunks - 1:
+                nc.sync.dma_start(out=c_rows[g][:, :, first:first + chunks * CHUNK], in_=c_sb[:])
 
         tol_sb = keep.tile([P, N], BF16, name="tol_sb", align_bytes=64)
 
@@ -165,85 +197,117 @@ def tile_checksum_verified_product_s7_kernel(tc, a, b, w, enc, parity, tol, out_
             nc.scalar.copy(out=tol_sb[:].bitcast(F32).rearrange("p (r x) -> p r x", x=4),
                            in_=bank[:].rearrange("p (x r) -> p r x", x=4))
 
-        def check_matmuls(h, j):
+        firsts = [sum(RANGES[:x]) * CHUNK for x in range(len(RANGES))]
+
+        def check_matmuls(x, j):
             bank = new_bank()
+            width = RANGES[x] * CHUNK
             for c in range(K_PASSES):
-                mx(bank[:], par_q[j // 2], ((j % 2) * K_PASSES + c) * P, b_q[h, c], 0, HALF, c == 0, False)
+                mx(bank[:, :width], par_q[j // 2], ((j % 2) * K_PASSES + c) * P, b_q[c],
+                   firsts[x], width, c == 0, False)
             for g in range(M_GROUPS):
-                mx(bank[:], enc_q[j], g * P, cw_q[g, h], 0, HALF, False, g == M_GROUPS - 1)
-            size = stage.tile([P, HALF], F32, name="size")
-            nc.scalar.activation(out=size[:], in_=bank[:], func=ACT.Abs)
+                mx(bank[:, :width], enc_q[j], g * P, cw_q[g, x], 0, width, False, g == M_GROUPS - 1)
+            return bank
+
+        def check_abs(bank, cols):
+            size = stage.tile([P, cols.stop - cols.start], F32, name="size")
+            nc.scalar.activation(out=size[:], in_=bank[:, cols], func=ACT.Abs)
             return size
 
-        def check_finish(h, j, size):
-            alarm = stage.tile([P, HALF], F32, name="alarm")
-            nc.vector.tensor_tensor(out=alarm[:], in0=size[:], in1=tol_sb[:, h * HALF:(h + 1) * HALF], op=ALU.max)
-            nc.sync.dma_start(out=out_1[j * P:(j + 1) * P, h * HALF:(h + 1) * HALF], in_=alarm[:])
+        def check_finish(x, j, size, cols):
+            alarm = stage.tile([P, cols.stop - cols.start], F32, name="alarm", bufs=6)
+            out_cols = slice(firsts[x] + cols.start, firsts[x] + cols.stop)
+            nc.vector.tensor_tensor(out=alarm[:], in0=size[:], in1=tol_sb[:, out_cols], op=ALU.max)
+            nc.sync.dma_start(out=out_1[j * P:(j + 1) * P, out_cols], in_=alarm[:])
 
-        ta0 = turn(a_src[0, 0])
-        gb0 = interleave(b_raw[0, 0])
+        ones = stage.tile([P, PACK * HALF], BF16, name="turned", align_bytes=64)
+        if sum(WARM):
+            nc.vector.memset(ones[:], 1.0)
+            idle = quantize("idle", ones)
+
+        def warm(count):
+            if count:
+                bank = new_bank()
+                for n in range(count):
+                    mx(bank[:], idle, 0, idle, 0, HALF, True, True)
+
+        warm(WARM[0])
+        ta0 = turn(stepped_words(a_src[0, 0]))
+        g00 = interleave(0, 0, 0, nc.vector.tensor_copy)
         a_q[0, 0] = quantize("a00", ta0)
-        b_q[0, 0] = quantize("b00", gb0)
-        ta1 = turn(a_src[0, 1])
-        gb1 = interleave(b_raw[0, 1])
+        quantize_b(0, 0, 0, g00)
+        warm(WARM[1])
+        ta1 = turn(stepped_words(a_src[0, 1]))
+        g10 = interleave(0, 1, 0, nc.vector.tensor_copy)
         a_q[0, 1] = quantize("a01", ta1)
-        b_q[0, 1] = quantize("b01", gb1)
+        quantize_b(0, 1, 0, g10)
         spread_tol()
+        warm(WARM[2])
 
-        def step(g, h, pair, pending, extra, early=0):
-            tiles = new_c_tiles()
-            for chunk in range(early):
-                product(g, h, chunk, tiles)
-            turned = [turn(x[3]) for x in pair]
-            for job in pending + extra:
-                job()
-            chunk = early
-            for x, grouped in zip(pair, turned):
-                x[0][x[1]] = quantize(x[2], grouped)
-                product(g, h, chunk, tiles)
-                chunk = chunk + 1
-            for rest in range(chunk, HALF // CHUNK):
-                product(g, h, rest, tiles)
+        units = [(a_q, (g, c), "a%d%d" % (g, c), a_src[g, c]) for g in range(1, M_GROUPS) for c in range(K_PASSES)]
+        for j in range(R_TILES):
+            units.append((enc_q, j, "enc%d" % j, enc_src[j]))
+            if j % 2 == 0:
+                units.append((par_q, j // 2, "par%d" % (j // 2), par_src[j // 2]))
+        copies = {"v": nc.vector.tensor_copy, "s": nc.scalar.copy, "g": nc.gpsimd.tensor_copy}
+        banks = [(x, g, chunk) for x in range(len(RANGES)) for g in range(M_GROUPS) for chunk in range(RANGES[x])]
+        checks = [(x, j) for x in range(len(RANGES)) for j in range(R_TILES)]
+        total = len(banks)
+        later = {i: [] for i in range(-4, total + 4)}
+        words = {}
 
-            def finish():
-                cw_q[g, h] = quantize("cw%d%d" % (g, h), tiles[1])
-            return [finish]
+        def defer(i, job, *args):
+            later[i].append((job, args))
 
-        def a_pair(g):
-            return [(a_q, (g, c), "a%d%d" % (g, c), a_src[g, c]) for c in range(K_PASSES)]
+        def quantize_into(store, key, name, grouped):
+            store[key] = quantize(name, grouped)
 
-        def enc_unit(j):
-            return (enc_q, j, "enc%d" % j, enc_src[j])
+        def sort_unit(n):
+            words[n] = sort_words(units[n][3], copies[SORT_BY[n]])
 
-        def par_unit(q):
-            return (par_q, q, "par%d" % q, par_src[q])
+        def b_part(i, h, c, q, copy):
+            defer(i + B_LAG, quantize_b, h, c, q, interleave(h, c, q, copy))
 
-        b_late = {}
+        for n, i in enumerate(TURN_AFTER):
+            if SORT_BY[n] == "n":
+                words[n] = stepped_words(units[n][3])
+            else:
+                defer(max(i - SORT_LEAD, -1), sort_unit, n)
+        for n, i in enumerate(B_AFTER):
+            defer(i, b_part, i, (n // 2 + 1) // 2, n % 2, (n // 2 + 1) % 2, copies[B_BY[n]])
 
-        def b_interleave(c):
-            def job():
-                b_late[c] = interleave(b_raw[1, c])
-            return job
+        for job, args in later[-1]:
+            job(*args)
+        for i, (x, g, chunk) in enumerate(banks):
+            if chunk == 0:
+                c_sb, cw = new_c_tiles(RANGES[x])
+            bank = product(g, firsts[x] + chunk * CHUNK)
+            if S_FIRST:
+                keep_c(g, firsts[x], chunk, RANGES[x], bank, c_sb)
+                weigh(g, chunk, bank, cw)
+            else:
+                weigh(g, chunk, bank, cw)
+                defer(i + C_LAG, keep_c, g, firsts[x], chunk, RANGES[x], bank, c_sb)
+            if chunk == RANGES[x] - 1:
+                defer(i + CWQ_LAG, quantize_into, cw_q, (g, x), "cw%d%d" % (g, x), cw)
+            for job, args in later[i]:
+                job(*args)
+            for n in range(len(units)):
+                if TURN_AFTER[n] == i:
+                    defer(i + TQ_LAG, quantize_into, units[n][0], units[n][1], units[n][2], turn(words[n]))
+            for n in range(len(CHECK_AFTER)):
+                if CHECK_AFTER[n] == i:
+                    whole = slice(0, RANGES[checks[n][0]] * CHUNK)
+                    defer(i + MAX_LAG, check_finish, *checks[n], check_abs(check_matmuls(*checks[n]), whole), whole)
 
-        def b_quantize(c):
-            def job():
-                b_q[1, c] = quantize("b1%d" % c, b_late[c])
-            return job
-
-        pending = step(0, 0, a_pair(1), [], [], early=2)
-        pending = step(1, 0, a_pair(2), pending, [b_interleave(0)])
-        pending = step(2, 0, a_pair(3), pending, [b_quantize(0), b_interleave(1)])
-        pending = step(3, 0, [enc_unit(0), par_unit(0)], pending, [b_quantize(1)])
-        pending = step(0, 1, [enc_unit(1), enc_unit(2)], pending, [])
-        size = check_matmuls(0, 0)
-        pending = step(1, 1, [], pending, [lambda: check_finish(0, 0, size)])
-        pending = step(2, 1, [enc_unit(3), par_unit(1)], pending, [])
-        size1 = check_matmuls(0, 1)
-        pending = step(3, 1, [], pending, [lambda: check_finish(0, 1, size1)])
-        rest = [(0, 2), (0, 3), (1, 0), (1, 1), (1, 2), (1, 3)]
-        for h, j in rest:
-            size2 = check_matmuls(h, j)
-            for job in pending:
-                job()
-            pending = []
-            check_finish(h, j, size2)
+        for i in range(total, total + 4):
+            for job, args in later[i]:
+                job(*args)
+        for x, j in checks[len(CHECK_AFTER):-1]:
+            whole = slice(0, RANGES[x] * CHUNK)
+            check_finish(x, j, check_abs(check_matmuls(x, j), whole), whole)
+        bank = check_matmuls(*checks[-1])
+        part = RANGES[-1] * CHUNK // 2
+        for q in range(2):
+            cols = slice(q * part, (q + 1) * part)
+            check_finish(*checks[-1], check_abs(bank, cols), cols)

@@ -17,27 +17,21 @@ ACT = mybir.ActivationFunctionType
 P = 128
 PACK = 4
 SPAN = P * PACK
-HALF = 512
-QUARTER = 256
-CHUNK = 128
+BANK = 512
 BANKS = 8
+CHUNK = BANK // PACK
+HALF = N // 2
+QUARTER = N // 4
 K_PASSES = K // SPAN
 M_GROUPS = M // SPAN
 R_TILES = R // P
+
 RANGES = (4, 2, 2)
-TURN_AFTER = [0, 1, 2, 4, 6, 8, 10, 12, 14, 16, 18, 20]
-SORT_BY = "nvnvnvnvnvnv"
-SORT_LEAD = 3
-TQ_LAG = 1
-CWQ_LAG = 1
-CHECK_AFTER = [19, 21, 23, 25, 27, 29]
-B_AFTER = [-1, -1, 6, 10, 18, 20]
-B_BY = "vvvvvv"
-B_LAG = 1
-S_FIRST = True
-C_LAG = 0
-MAX_LAG = 2
-WARM = [4, 4, 3]
+SORT_EVERY = 4
+SORT_LEAD = 2
+UNIT_STEP = 2
+SIDE_STEP = 4
+WARM_PASSES = 8
 
 
 def tile_checksum_verified_product_s7_kernel(tc, a, b, w, enc, parity, tol, out_0, out_1):
@@ -48,86 +42,87 @@ def tile_checksum_verified_product_s7_kernel(tc, a, b, w, enc, parity, tol, out_
         psum = ctx.enter_context(tc.psum_pool(name="psum", bufs=1))
         ctx.enter_context(tc.manual_schedule())
 
-        taken = []
+        banks_taken = []
 
         def new_bank():
-            name = "bank%d" % (len(taken) % BANKS)
-            taken.append(name)
-            return psum.tile([P, HALF], F32, name=name)
+            name = "bank%d" % (len(banks_taken) % BANKS)
+            banks_taken.append(name)
+            return psum.tile([P, BANK], F32, name=name)
 
         def load(name, shape, source, engine):
-            t = keep.tile(shape, BF16, name=name, align_bytes=64)
-            engine.dma_start(out=t[:], in_=source)
-            return t
+            tile = keep.tile(shape, BF16, name=name, align_bytes=64)
+            engine.dma_start(out=tile[:], in_=source)
+            return tile
 
-        def operand(name, width=HALF):
+        def new_operand(name, width):
             codes = keep.tile([P, width], U32, name=name + "_codes", align_bytes=64)
             scales = keep.tile([P, width], U8, name=name + "_scales", align_bytes=64)
             return codes, scales
 
         def quantize(name, grouped):
-            codes, scales = operand(name, grouped.shape[1] // PACK)
+            codes, scales = new_operand(name, grouped.shape[1] // PACK)
             nc.vector.quantize_mx(out=codes[:].bitcast(FP8X4), scales=scales[:], in_=grouped[:])
             return codes, scales
 
         def mx(out, lhs, lhs_at, rhs, rhs_at, width, start, stop):
-            lc = slice(lhs_at, lhs_at + P)
-            rc = slice(rhs_at, rhs_at + width)
+            lhs_cols = slice(lhs_at, lhs_at + P)
+            rhs_cols = slice(rhs_at, rhs_at + width)
             nc.tensor.matmul_mx(
                 out=out,
-                lhsT=lhs[0][:, lc].bitcast(FP8X4), lhsT_scale=lhs[1][:, lc],
-                rhs=rhs[0][:, rc].bitcast(FP8X4), rhs_scale=rhs[1][:, rc],
+                lhsT=lhs[0][:, lhs_cols].bitcast(FP8X4), lhsT_scale=lhs[1][:, lhs_cols],
+                rhs=rhs[0][:, rhs_cols].bitcast(FP8X4), rhs_scale=rhs[1][:, rhs_cols],
                 start=start, stop=stop,
             )
 
         a_rows = a.rearrange("(g p t) k -> g p t k", p=P, t=PACK)
-        b_rows = b.rearrange("(c p j) n -> c p j n", p=P, j=PACK)
-        w_sb = load("w_sb", [P, M_GROUPS, PACK], w.rearrange("(g p t) -> p g t", p=P, t=PACK), nc.scalar)
-        tol_cols = load("tol_cols", [P, N // P], tol.rearrange("(p x) -> p x", p=P), nc.scalar)
-
+        b_rows = b.rearrange("(s p t) n -> s p t n", p=P, t=PACK)
+        parity_rows = parity.rearrange("(q x p) k -> q p x k", p=P, x=2)
         a_src = {}
         b_raw = {}
-
-        def load_b(h, c):
-            b_raw[h, c] = load("b_raw%d%d" % (h, c), [P, PACK, HALF], b_rows[c][:, :, h * HALF:(h + 1) * HALF], nc.sync)
-
-        for c in range(K_PASSES):
-            t0 = load("a_raw0%d" % c, [P, PACK, SPAN], a_rows[0][:, :, c * SPAN:(c + 1) * SPAN], nc.sync)
-            a_src[0, c] = t0[:]
-            load_b(0, c)
-        for g in range(1, M_GROUPS):
-            tg = load("a_raw%d" % g, [P, PACK, K], a_rows[g], nc.sync)
-            for c in range(K_PASSES):
-                a_src[g, c] = tg[:, :, c * SPAN:(c + 1) * SPAN]
-        for c in range(K_PASSES):
-            load_b(1, c)
         enc_src = {}
-        par_src = {}
-        par_rows = parity.rearrange("(q j p) k -> q p j k", p=P, j=2)
+        parity_src = {}
+
+        def load_a(g, y):
+            raw = load("a_raw%d%d" % (g, y), [P, 2, K], a_rows[g][:, 2 * y:2 * y + 2, :], nc.sync)
+            a_src[g, y] = raw[:].rearrange("p x (s k) -> p (x s) k", k=SPAN)
+
+        def load_b(h, s):
+            b_raw[h, s] = load("b_raw%d%d" % (h, s), [P, PACK, HALF], b_rows[s][:, :, h * HALF:(h + 1) * HALF], nc.sync)
+
+        for y in range(2):
+            load_a(0, y)
+            load_b(0, y)
+        w_sb = load("w_sb", [P, M_GROUPS, PACK], w.rearrange("(g p t) -> p g t", p=P, t=PACK), nc.scalar)
+        tol_cols = load("tol_cols", [P, N // P], tol.rearrange("(p x) -> p x", p=P), nc.scalar)
+        for g in range(1, M_GROUPS):
+            for y in range(2):
+                load_a(g, y)
+        for s in range(K_PASSES):
+            load_b(1, s)
         for j in range(R_TILES):
-            te = load("enc_raw%d" % j, [P, M], enc[j * P:(j + 1) * P, :], nc.sync)
-            enc_src[j] = te[:].rearrange("p (g k) -> p g k", k=SPAN)
+            raw = load("enc_raw%d" % j, [P, M], enc[j * P:(j + 1) * P, :], nc.sync)
+            enc_src[j] = raw[:].rearrange("p (s k) -> p s k", k=SPAN)
             if j % 2 == 0:
-                tp = load("par_raw%d" % (j // 2), [P, 2, K], par_rows[j // 2], nc.sync)
-                par_src[j // 2] = tp[:].rearrange("p x (c k) -> p (x c) k", k=SPAN)
+                raw = load("parity_raw%d" % (j // 2), [P, 2, K], parity_rows[j // 2], nc.sync)
+                parity_src[j // 2] = raw[:].rearrange("p x (s k) -> p (x s) k", k=SPAN)
 
         ident = keep.tile([P, P], F32, name="ident")
         make_identity(nc, ident[:])
         ident_abs = keep.tile([P, P], F32, name="ident_abs")
         nc.scalar.activation(out=ident_abs[:], in_=ident[:], func=ACT.Abs)
 
-        def sort_words(source, copy):
-            ordered = stage.tile([P, PACK, 2, P], F32, name="ordered", bufs=3)
-            copy(out=ordered[:], in_=source.bitcast(F32).rearrange("p s (x u) -> p s u x", u=2))
-            return [[ordered[:, s, u, :] for u in range(2)] for s in range(PACK)]
-
         def stepped_words(source):
             words = source.bitcast(F32)
             return [[words[:, s, u:2 * P:2] for u in range(2)] for s in range(PACK)]
 
+        def sorted_words(source):
+            ordered = stage.tile([P, PACK, 2, P], F32, name="ordered", bufs=2)
+            nc.vector.tensor_copy(out=ordered[:], in_=source.bitcast(F32).rearrange("p s (x u) -> p s u x", u=2))
+            return [[ordered[:, s, u, :] for u in range(2)] for s in range(PACK)]
+
         def turn(words):
-            grouped = stage.tile([P, PACK * SPAN], BF16, name="turned", align_bytes=64)
-            words_out = grouped[:].bitcast(F32)
+            turned = stage.tile([P, PACK * SPAN], BF16, name="turned", align_bytes=64)
+            turned_words = turned[:].bitcast(F32)
             for pair in range(2):
                 bank = new_bank()
                 for x in range(2):
@@ -135,57 +130,55 @@ def tile_checksum_verified_product_s7_kernel(tc, a, b, w, enc, parity, tol, out_
                         at = (2 * x + u) * P
                         nc.tensor.transpose(bank[:, at:at + P], words[2 * pair + x][u], ident[:])
                 nc.scalar.copy(
-                    out=words_out[:, pair * HALF:(pair + 1) * HALF].rearrange("p (x r u) -> p x r u", x=2, u=2),
+                    out=turned_words[:, pair * BANK:(pair + 1) * BANK].rearrange("p (x r u) -> p x r u", x=2, u=2),
                     in_=bank[:].rearrange("p (x u r) -> p x r u", x=2, u=2),
                 )
-            return grouped
+            return turned
 
-        def interleave(h, c, q, copy):
+        b_q = {s: new_operand("b%d" % s, N) for s in range(K_PASSES)}
+
+        def interleave_b(s, q, copy):
             grouped = stage.tile([P, PACK * QUARTER], BF16, name="b_grouped", align_bytes=64, bufs=4)
+            at = (q % 2) * QUARTER
             copy(
-                out=grouped[:].rearrange("p (c i t) -> p c t i", i=4, t=PACK),
-                in_=b_raw[h, c][:, :, q * QUARTER:(q + 1) * QUARTER].rearrange("p t (c i) -> p c t i", i=4),
+                out=grouped[:].rearrange("p (n i t) -> p n t i", i=4, t=PACK),
+                in_=b_raw[q // 2, s][:, :, at:at + QUARTER].rearrange("p t (n i) -> p n t i", i=4),
             )
             return grouped
 
-        def quantize_b(h, c, q, grouped):
-            codes, scales = b_q[c]
-            cols = slice((2 * h + q) * QUARTER, (2 * h + q + 1) * QUARTER)
+        def quantize_b(s, q, grouped):
+            codes, scales = b_q[s]
+            cols = slice(q * QUARTER, (q + 1) * QUARTER)
             nc.vector.quantize_mx(out=codes[:, cols].bitcast(FP8X4), scales=scales[:, cols], in_=grouped[:])
 
         a_q = {}
-        b_q = {c: operand("b%d" % c, N) for c in range(K_PASSES)}
         enc_q = {}
-        par_q = {}
+        parity_q = {}
         cw_q = {}
         c_rows = out_0.rearrange("(g p t) n -> g p t n", p=P, t=PACK)
-
-        def new_c_tiles(chunks):
-            c_sb = stage.tile([P, PACK, chunks * CHUNK], F32, name="c_sb", bufs=4)
-            cw = stage.tile([P, PACK * chunks * CHUNK], BF16, name="cw", align_bytes=64, bufs=2)
-            return c_sb, cw
+        range_at = [sum(RANGES[:x]) * CHUNK for x in range(len(RANGES))]
 
         def product(g, col):
             bank = new_bank()
             for t in range(PACK):
-                for c in range(K_PASSES):
-                    mx(bank[:, t * CHUNK:(t + 1) * CHUNK], a_q[g, c], t * P, b_q[c], col, CHUNK,
-                       c == 0, c == K_PASSES - 1)
+                for s in range(K_PASSES):
+                    mx(bank[:, t * CHUNK:(t + 1) * CHUNK], a_q[g, t // 2], ((t % 2) * K_PASSES + s) * P,
+                       b_q[s], col, CHUNK, s == 0, s == K_PASSES - 1)
             return bank
 
         def weigh(g, chunk, bank, cw):
             nc.vector.tensor_tensor(
-                out=cw[:, chunk * HALF:(chunk + 1) * HALF].rearrange("p (n t) -> p n t", t=PACK),
+                out=cw[:, chunk * BANK:(chunk + 1) * BANK].rearrange("p (n t) -> p n t", t=PACK),
                 in0=bank[:].rearrange("p (t n) -> p n t", t=PACK),
                 in1=w_sb[:, g:g + 1, :].to_broadcast([P, CHUNK, PACK]),
                 op=ALU.mult,
             )
 
-        def keep_c(g, first, chunk, chunks, bank, c_sb):
+        def keep_c(x, g, chunk, bank, c_sb):
             nc.scalar.copy(out=c_sb[:, :, chunk * CHUNK:(chunk + 1) * CHUNK],
                            in_=bank[:].rearrange("p (t n) -> p t n", t=PACK))
-            if chunk == chunks - 1:
-                nc.sync.dma_start(out=c_rows[g][:, :, first:first + chunks * CHUNK], in_=c_sb[:])
+            if chunk == RANGES[x] - 1:
+                nc.sync.dma_start(out=c_rows[g][:, :, range_at[x]:range_at[x] + RANGES[x] * CHUNK], in_=c_sb[:])
 
         tol_sb = keep.tile([P, N], BF16, name="tol_sb", align_bytes=64)
 
@@ -197,64 +190,54 @@ def tile_checksum_verified_product_s7_kernel(tc, a, b, w, enc, parity, tol, out_
             nc.scalar.copy(out=tol_sb[:].bitcast(F32).rearrange("p (r x) -> p r x", x=4),
                            in_=bank[:].rearrange("p (x r) -> p r x", x=4))
 
-        firsts = [sum(RANGES[:x]) * CHUNK for x in range(len(RANGES))]
-
-        def check_matmuls(x, j):
+        def discrepancy(x, j):
             bank = new_bank()
             width = RANGES[x] * CHUNK
-            for c in range(K_PASSES):
-                mx(bank[:, :width], par_q[j // 2], ((j % 2) * K_PASSES + c) * P, b_q[c],
-                   firsts[x], width, c == 0, False)
+            for s in range(K_PASSES):
+                mx(bank[:, :width], parity_q[j // 2], ((j % 2) * K_PASSES + s) * P, b_q[s], range_at[x], width,
+                   s == 0, False)
             for g in range(M_GROUPS):
                 mx(bank[:, :width], enc_q[j], g * P, cw_q[g, x], 0, width, False, g == M_GROUPS - 1)
             return bank
 
-        def check_abs(bank, cols):
+        def magnitude(bank, cols):
             size = stage.tile([P, cols.stop - cols.start], F32, name="size")
             nc.scalar.activation(out=size[:], in_=bank[:, cols], func=ACT.Abs)
             return size
 
-        def check_finish(x, j, size, cols):
-            alarm = stage.tile([P, cols.stop - cols.start], F32, name="alarm", bufs=6)
-            out_cols = slice(firsts[x] + cols.start, firsts[x] + cols.stop)
+        def threshold(x, j, size, cols):
+            alarm = stage.tile([P, cols.stop - cols.start], F32, name="alarm", bufs=8)
+            out_cols = slice(range_at[x] + cols.start, range_at[x] + cols.stop)
             nc.vector.tensor_tensor(out=alarm[:], in0=size[:], in1=tol_sb[:, out_cols], op=ALU.max)
             nc.sync.dma_start(out=out_1[j * P:(j + 1) * P, out_cols], in_=alarm[:])
 
-        ones = stage.tile([P, PACK * HALF], BF16, name="turned", align_bytes=64)
-        if sum(WARM):
-            nc.vector.memset(ones[:], 1.0)
-            idle = quantize("idle", ones)
+        zeros = keep.tile([P, PACK * QUARTER], BF16, name="zeros", align_bytes=64)
+        nc.vector.memset(zeros[:], 0.0)
+        zeros_q = quantize("zeros", zeros)
 
-        def warm(count):
-            if count:
-                bank = new_bank()
-                for n in range(count):
-                    mx(bank[:], idle, 0, idle, 0, HALF, True, True)
+        def warm_up():
+            bank = new_bank()
+            for n in range(WARM_PASSES):
+                mx(bank[:, :QUARTER], zeros_q, 0, zeros_q, 0, QUARTER, True, True)
 
-        warm(WARM[0])
-        ta0 = turn(stepped_words(a_src[0, 0]))
-        g00 = interleave(0, 0, 0, nc.vector.tensor_copy)
-        a_q[0, 0] = quantize("a00", ta0)
-        quantize_b(0, 0, 0, g00)
-        warm(WARM[1])
-        ta1 = turn(stepped_words(a_src[0, 1]))
-        g10 = interleave(0, 1, 0, nc.vector.tensor_copy)
-        a_q[0, 1] = quantize("a01", ta1)
-        quantize_b(0, 1, 0, g10)
-        spread_tol()
-        warm(WARM[2])
+        warm_up()
+        turned_a00 = turn(stepped_words(a_src[0, 0]))
+        grouped_b00 = interleave_b(0, 0, nc.vector.tensor_copy)
+        a_q[0, 0] = quantize("a00", turned_a00)
+        quantize_b(0, 0, grouped_b00)
+        grouped_b01 = interleave_b(0, 1, nc.scalar.copy)
+        warm_up()
+        turned_a01 = turn(stepped_words(a_src[0, 1]))
+        grouped_b10 = interleave_b(1, 0, nc.vector.tensor_copy)
+        quantize_b(0, 1, grouped_b01)
+        quantize_b(1, 0, grouped_b10)
+        a_q[0, 1] = quantize("a01", turned_a01)
+        grouped_b11 = interleave_b(1, 1, nc.vector.tensor_copy)
+        warm_up()
 
-        units = [(a_q, (g, c), "a%d%d" % (g, c), a_src[g, c]) for g in range(1, M_GROUPS) for c in range(K_PASSES)]
-        for j in range(R_TILES):
-            units.append((enc_q, j, "enc%d" % j, enc_src[j]))
-            if j % 2 == 0:
-                units.append((par_q, j // 2, "par%d" % (j // 2), par_src[j // 2]))
-        copies = {"v": nc.vector.tensor_copy, "s": nc.scalar.copy, "g": nc.gpsimd.tensor_copy}
-        banks = [(x, g, chunk) for x in range(len(RANGES)) for g in range(M_GROUPS) for chunk in range(RANGES[x])]
+        c_banks = [(x, g, chunk) for x in range(len(RANGES)) for g in range(M_GROUPS) for chunk in range(RANGES[x])]
         checks = [(x, j) for x in range(len(RANGES)) for j in range(R_TILES)]
-        total = len(banks)
-        later = {i: [] for i in range(-4, total + 4)}
-        words = {}
+        later = {i: [] for i in range(len(c_banks) + 1)}
 
         def defer(i, job, *args):
             later[i].append((job, args))
@@ -262,52 +245,62 @@ def tile_checksum_verified_product_s7_kernel(tc, a, b, w, enc, parity, tol, out_
         def quantize_into(store, key, name, grouped):
             store[key] = quantize(name, grouped)
 
+        units = [(a_q, (g, y), "a%d%d" % (g, y), a_src[g, y]) for g in range(1, M_GROUPS) for y in range(2)]
+        for j in range(R_TILES):
+            units.append((enc_q, j, "enc%d" % j, enc_src[j]))
+            if j % 2 == 0:
+                units.append((parity_q, j // 2, "parity%d" % (j // 2), parity_src[j // 2]))
+        unit_after = {UNIT_STEP * (n - 1): n for n in range(1, len(units))}
+        tol_after = UNIT_STEP * (2 * SORT_EVERY - 2)
+        unit_words = {}
+
         def sort_unit(n):
-            words[n] = sort_words(units[n][3], copies[SORT_BY[n]])
+            unit_words[n] = sorted_words(units[n][3])
 
-        def b_part(i, h, c, q, copy):
-            defer(i + B_LAG, quantize_b, h, c, q, interleave(h, c, q, copy))
+        def turn_unit(n, i):
+            store, key, name, source = units[n]
+            words = unit_words[n] if n in unit_words else stepped_words(source)
+            defer(i + 1, quantize_into, store, key, name, turn(words))
 
-        for n, i in enumerate(TURN_AFTER):
-            if SORT_BY[n] == "n":
-                words[n] = stepped_words(units[n][3])
-            else:
-                defer(max(i - SORT_LEAD, -1), sort_unit, n)
-        for n, i in enumerate(B_AFTER):
-            defer(i, b_part, i, (n // 2 + 1) // 2, n % 2, (n // 2 + 1) % 2, copies[B_BY[n]])
+        def late_b(i, s, q):
+            defer(i + 1, quantize_b, s, q, interleave_b(s, q, nc.vector.tensor_copy))
 
-        for job, args in later[-1]:
-            job(*args)
-        for i, (x, g, chunk) in enumerate(banks):
+        defer(0, quantize_b, 1, 1, grouped_b11)
+        for n in range(SORT_EVERY - 1, len(units), SORT_EVERY):
+            defer(UNIT_STEP * (n - 1) - SORT_LEAD, sort_unit, n)
+        for n in range(2 * K_PASSES):
+            i = SIDE_STEP * (n + 2) - 1
+            defer(i, late_b, i, n % K_PASSES, 2 + n // K_PASSES)
+        check_after = range(M_GROUPS * RANGES[0] + SIDE_STEP - 1, len(c_banks), SIDE_STEP)
+
+        turn_unit(0, -1)
+        for i, (x, g, chunk) in enumerate(c_banks):
             if chunk == 0:
-                c_sb, cw = new_c_tiles(RANGES[x])
-            bank = product(g, firsts[x] + chunk * CHUNK)
-            if S_FIRST:
-                keep_c(g, firsts[x], chunk, RANGES[x], bank, c_sb)
-                weigh(g, chunk, bank, cw)
-            else:
-                weigh(g, chunk, bank, cw)
-                defer(i + C_LAG, keep_c, g, firsts[x], chunk, RANGES[x], bank, c_sb)
+                c_sb = stage.tile([P, PACK, RANGES[x] * CHUNK], F32, name="c_sb", bufs=4)
+                cw = stage.tile([P, RANGES[x] * BANK], BF16, name="cw", align_bytes=64, bufs=2)
+            bank = product(g, range_at[x] + chunk * CHUNK)
+            weigh(g, chunk, bank, cw)
+            defer(i + 1, keep_c, x, g, chunk, bank, c_sb)
             if chunk == RANGES[x] - 1:
-                defer(i + CWQ_LAG, quantize_into, cw_q, (g, x), "cw%d%d" % (g, x), cw)
+                defer(i + 1, quantize_into, cw_q, (g, x), "cw%d%d" % (g, x), cw)
             for job, args in later[i]:
                 job(*args)
-            for n in range(len(units)):
-                if TURN_AFTER[n] == i:
-                    defer(i + TQ_LAG, quantize_into, units[n][0], units[n][1], units[n][2], turn(words[n]))
-            for n in range(len(CHECK_AFTER)):
-                if CHECK_AFTER[n] == i:
-                    whole = slice(0, RANGES[checks[n][0]] * CHUNK)
-                    defer(i + MAX_LAG, check_finish, *checks[n], check_abs(check_matmuls(*checks[n]), whole), whole)
+            if i in unit_after:
+                turn_unit(unit_after[i], i)
+            if i == tol_after:
+                spread_tol()
+            if i in check_after:
+                check = checks[check_after.index(i)]
+                whole = slice(0, RANGES[check[0]] * CHUNK)
+                defer(i + 1, threshold, *check, magnitude(discrepancy(*check), whole), whole)
 
-        for i in range(total, total + 4):
-            for job, args in later[i]:
-                job(*args)
-        for x, j in checks[len(CHECK_AFTER):-1]:
+        for job, args in later[len(c_banks)]:
+            job(*args)
+        for x, j in checks[len(check_after):-1]:
             whole = slice(0, RANGES[x] * CHUNK)
-            check_finish(x, j, check_abs(check_matmuls(x, j), whole), whole)
-        bank = check_matmuls(*checks[-1])
+            threshold(x, j, magnitude(discrepancy(x, j), whole), whole)
+        bank = discrepancy(*checks[-1])
         part = RANGES[-1] * CHUNK // 2
-        for q in range(2):
-            cols = slice(q * part, (q + 1) * part)
-            check_finish(*checks[-1], check_abs(bank, cols), cols)
+        for n in range(2):
+            cols = slice(n * part, (n + 1) * part)
+            threshold(*checks[-1], magnitude(bank, cols), cols)

from contextlib import ExitStack

import concourse.mybir as mybir
from concourse.masks import make_identity

M, K, N, R = 2048, 1024, 1024, 512
FLOPS = 2 * M * K * N + 2 * R * M * N + 2 * R * K * N

F32 = mybir.dt.float32
BF16 = mybir.dt.bfloat16
U32 = mybir.dt.uint32
U8 = mybir.dt.uint8
FP8X4 = mybir.dt.float8_e4m3fn_x4
ALU = mybir.AluOpType
ACT = mybir.ActivationFunctionType

P = 128
PACK = 4
SPAN = P * PACK
BANK = 512
BANKS = 8
CHUNK = BANK // PACK
HALF = N // 2
QUARTER = N // 4
K_PASSES = K // SPAN
M_GROUPS = M // SPAN
R_TILES = R // P

RANGES = (4, 2, 2)
SORT_EVERY = 4
SORT_LEAD = 2
UNIT_STEP = 2
SIDE_STEP = 4
WARM_PASSES = 8


def tile_checksum_verified_product_s7_kernel(tc, a, b, w, enc, parity, tol, out_0, out_1):
    nc = tc.nc
    with ExitStack() as ctx:
        keep = ctx.enter_context(tc.tile_pool(name="keep", bufs=1))
        stage = ctx.enter_context(tc.tile_pool(name="stage", bufs=3))
        psum = ctx.enter_context(tc.psum_pool(name="psum", bufs=1))
        ctx.enter_context(tc.manual_schedule())

        banks_taken = []

        def new_bank():
            name = "bank%d" % (len(banks_taken) % BANKS)
            banks_taken.append(name)
            return psum.tile([P, BANK], F32, name=name)

        def load(name, shape, source, engine):
            tile = keep.tile(shape, BF16, name=name, align_bytes=64)
            engine.dma_start(out=tile[:], in_=source)
            return tile

        def new_operand(name, width):
            codes = keep.tile([P, width], U32, name=name + "_codes", align_bytes=64)
            scales = keep.tile([P, width], U8, name=name + "_scales", align_bytes=64)
            return codes, scales

        def quantize(name, grouped):
            codes, scales = new_operand(name, grouped.shape[1] // PACK)
            nc.vector.quantize_mx(out=codes[:].bitcast(FP8X4), scales=scales[:], in_=grouped[:])
            return codes, scales

        def mx(out, lhs, lhs_at, rhs, rhs_at, width, start, stop):
            lhs_cols = slice(lhs_at, lhs_at + P)
            rhs_cols = slice(rhs_at, rhs_at + width)
            nc.tensor.matmul_mx(
                out=out,
                lhsT=lhs[0][:, lhs_cols].bitcast(FP8X4), lhsT_scale=lhs[1][:, lhs_cols],
                rhs=rhs[0][:, rhs_cols].bitcast(FP8X4), rhs_scale=rhs[1][:, rhs_cols],
                start=start, stop=stop,
            )

        a_rows = a.rearrange("(g p t) k -> g p t k", p=P, t=PACK)
        b_rows = b.rearrange("(s p t) n -> s p t n", p=P, t=PACK)
        parity_rows = parity.rearrange("(q x p) k -> q p x k", p=P, x=2)
        a_src = {}
        b_raw = {}
        enc_src = {}
        parity_src = {}

        def load_a(g, y):
            raw = load("a_raw%d%d" % (g, y), [P, 2, K], a_rows[g][:, 2 * y:2 * y + 2, :], nc.sync)
            a_src[g, y] = raw[:].rearrange("p x (s k) -> p (x s) k", k=SPAN)

        def load_b(h, s):
            b_raw[h, s] = load("b_raw%d%d" % (h, s), [P, PACK, HALF], b_rows[s][:, :, h * HALF:(h + 1) * HALF], nc.sync)

        for y in range(2):
            load_a(0, y)
            load_b(0, y)
        w_sb = load("w_sb", [P, M_GROUPS, PACK], w.rearrange("(g p t) -> p g t", p=P, t=PACK), nc.scalar)
        tol_cols = load("tol_cols", [P, N // P], tol.rearrange("(p x) -> p x", p=P), nc.scalar)
        for g in range(1, M_GROUPS):
            for y in range(2):
                load_a(g, y)
        for s in range(K_PASSES):
            load_b(1, s)
        for j in range(R_TILES):
            raw = load("enc_raw%d" % j, [P, M], enc[j * P:(j + 1) * P, :], nc.sync)
            enc_src[j] = raw[:].rearrange("p (s k) -> p s k", k=SPAN)
            if j % 2 == 0:
                raw = load("parity_raw%d" % (j // 2), [P, 2, K], parity_rows[j // 2], nc.sync)
                parity_src[j // 2] = raw[:].rearrange("p x (s k) -> p (x s) k", k=SPAN)

        ident = keep.tile([P, P], F32, name="ident")
        make_identity(nc, ident[:])
        ident_abs = keep.tile([P, P], F32, name="ident_abs")
        nc.scalar.activation(out=ident_abs[:], in_=ident[:], func=ACT.Abs)

        def stepped_words(source):
            words = source.bitcast(F32)
            return [[words[:, s, u:2 * P:2] for u in range(2)] for s in range(PACK)]

        def sorted_words(source):
            ordered = stage.tile([P, PACK, 2, P], F32, name="ordered", bufs=2)
            nc.vector.tensor_copy(out=ordered[:], in_=source.bitcast(F32).rearrange("p s (x u) -> p s u x", u=2))
            return [[ordered[:, s, u, :] for u in range(2)] for s in range(PACK)]

        def turn(words):
            turned = stage.tile([P, PACK * SPAN], BF16, name="turned", align_bytes=64)
            turned_words = turned[:].bitcast(F32)
            for pair in range(2):
                bank = new_bank()
                for x in range(2):
                    for u in range(2):
                        at = (2 * x + u) * P
                        nc.tensor.transpose(bank[:, at:at + P], words[2 * pair + x][u], ident[:])
                nc.scalar.copy(
                    out=turned_words[:, pair * BANK:(pair + 1) * BANK].rearrange("p (x r u) -> p x r u", x=2, u=2),
                    in_=bank[:].rearrange("p (x u r) -> p x r u", x=2, u=2),
                )
            return turned

        b_q = {s: new_operand("b%d" % s, N) for s in range(K_PASSES)}

        def interleave_b(s, q, copy):
            grouped = stage.tile([P, PACK * QUARTER], BF16, name="b_grouped", align_bytes=64, bufs=4)
            at = (q % 2) * QUARTER
            copy(
                out=grouped[:].rearrange("p (n i t) -> p n t i", i=4, t=PACK),
                in_=b_raw[q // 2, s][:, :, at:at + QUARTER].rearrange("p t (n i) -> p n t i", i=4),
            )
            return grouped

        def quantize_b(s, q, grouped):
            codes, scales = b_q[s]
            cols = slice(q * QUARTER, (q + 1) * QUARTER)
            nc.vector.quantize_mx(out=codes[:, cols].bitcast(FP8X4), scales=scales[:, cols], in_=grouped[:])

        a_q = {}
        enc_q = {}
        parity_q = {}
        cw_q = {}
        c_rows = out_0.rearrange("(g p t) n -> g p t n", p=P, t=PACK)
        range_at = [sum(RANGES[:x]) * CHUNK for x in range(len(RANGES))]

        def product(g, col):
            bank = new_bank()
            for t in range(PACK):
                for s in range(K_PASSES):
                    mx(bank[:, t * CHUNK:(t + 1) * CHUNK], a_q[g, t // 2], ((t % 2) * K_PASSES + s) * P,
                       b_q[s], col, CHUNK, s == 0, s == K_PASSES - 1)
            return bank

        def weigh(g, chunk, bank, cw):
            nc.vector.tensor_tensor(
                out=cw[:, chunk * BANK:(chunk + 1) * BANK].rearrange("p (n t) -> p n t", t=PACK),
                in0=bank[:].rearrange("p (t n) -> p n t", t=PACK),
                in1=w_sb[:, g:g + 1, :].to_broadcast([P, CHUNK, PACK]),
                op=ALU.mult,
            )

        def keep_c(x, g, chunk, bank, c_sb):
            nc.scalar.copy(out=c_sb[:, :, chunk * CHUNK:(chunk + 1) * CHUNK],
                           in_=bank[:].rearrange("p (t n) -> p t n", t=PACK))
            if chunk == RANGES[x] - 1:
                nc.sync.dma_start(out=c_rows[g][:, :, range_at[x]:range_at[x] + RANGES[x] * CHUNK], in_=c_sb[:])

        tol_sb = keep.tile([P, N], BF16, name="tol_sb", align_bytes=64)

        def spread_tol():
            bank = new_bank()
            words = tol_cols[:].bitcast(F32)
            for x in range(4):
                nc.tensor.transpose(bank[:, x * P:(x + 1) * P], words[:, x:x + 1].to_broadcast([P, P]), ident_abs[:])
            nc.scalar.copy(out=tol_sb[:].bitcast(F32).rearrange("p (r x) -> p r x", x=4),
                           in_=bank[:].rearrange("p (x r) -> p r x", x=4))

        def discrepancy(x, j):
            bank = new_bank()
            width = RANGES[x] * CHUNK
            for s in range(K_PASSES):
                mx(bank[:, :width], parity_q[j // 2], ((j % 2) * K_PASSES + s) * P, b_q[s], range_at[x], width,
                   s == 0, False)
            for g in range(M_GROUPS):
                mx(bank[:, :width], enc_q[j], g * P, cw_q[g, x], 0, width, False, g == M_GROUPS - 1)
            return bank

        def magnitude(bank, cols):
            size = stage.tile([P, cols.stop - cols.start], F32, name="size")
            nc.scalar.activation(out=size[:], in_=bank[:, cols], func=ACT.Abs)
            return size

        def threshold(x, j, size, cols):
            alarm = stage.tile([P, cols.stop - cols.start], F32, name="alarm", bufs=8)
            out_cols = slice(range_at[x] + cols.start, range_at[x] + cols.stop)
            nc.vector.tensor_tensor(out=alarm[:], in0=size[:], in1=tol_sb[:, out_cols], op=ALU.max)
            nc.sync.dma_start(out=out_1[j * P:(j + 1) * P, out_cols], in_=alarm[:])

        zeros = keep.tile([P, PACK * QUARTER], BF16, name="zeros", align_bytes=64)
        nc.vector.memset(zeros[:], 0.0)
        zeros_q = quantize("zeros", zeros)

        def warm_up():
            bank = new_bank()
            for n in range(WARM_PASSES):
                mx(bank[:, :QUARTER], zeros_q, 0, zeros_q, 0, QUARTER, True, True)

        warm_up()
        turned_a00 = turn(stepped_words(a_src[0, 0]))
        grouped_b00 = interleave_b(0, 0, nc.vector.tensor_copy)
        a_q[0, 0] = quantize("a00", turned_a00)
        quantize_b(0, 0, grouped_b00)
        grouped_b01 = interleave_b(0, 1, nc.scalar.copy)
        warm_up()
        turned_a01 = turn(stepped_words(a_src[0, 1]))
        grouped_b10 = interleave_b(1, 0, nc.vector.tensor_copy)
        quantize_b(0, 1, grouped_b01)
        quantize_b(1, 0, grouped_b10)
        a_q[0, 1] = quantize("a01", turned_a01)
        grouped_b11 = interleave_b(1, 1, nc.vector.tensor_copy)
        warm_up()

        c_banks = [(x, g, chunk) for x in range(len(RANGES)) for g in range(M_GROUPS) for chunk in range(RANGES[x])]
        checks = [(x, j) for x in range(len(RANGES)) for j in range(R_TILES)]
        later = {i: [] for i in range(len(c_banks) + 1)}

        def defer(i, job, *args):
            later[i].append((job, args))

        def quantize_into(store, key, name, grouped):
            store[key] = quantize(name, grouped)

        units = [(a_q, (g, y), "a%d%d" % (g, y), a_src[g, y]) for g in range(1, M_GROUPS) for y in range(2)]
        for j in range(R_TILES):
            units.append((enc_q, j, "enc%d" % j, enc_src[j]))
            if j % 2 == 0:
                units.append((parity_q, j // 2, "parity%d" % (j // 2), parity_src[j // 2]))
        unit_after = {UNIT_STEP * (n - 1): n for n in range(1, len(units))}
        tol_after = UNIT_STEP * (2 * SORT_EVERY - 2)
        unit_words = {}

        def sort_unit(n):
            unit_words[n] = sorted_words(units[n][3])

        def turn_unit(n, i):
            store, key, name, source = units[n]
            words = unit_words[n] if n in unit_words else stepped_words(source)
            defer(i + 1, quantize_into, store, key, name, turn(words))

        def late_b(i, s, q):
            defer(i + 1, quantize_b, s, q, interleave_b(s, q, nc.vector.tensor_copy))

        defer(0, quantize_b, 1, 1, grouped_b11)
        for n in range(SORT_EVERY - 1, len(units), SORT_EVERY):
            defer(UNIT_STEP * (n - 1) - SORT_LEAD, sort_unit, n)
        for n in range(2 * K_PASSES):
            i = SIDE_STEP * (n + 2) - 1
            defer(i, late_b, i, n % K_PASSES, 2 + n // K_PASSES)
        check_after = range(M_GROUPS * RANGES[0] + SIDE_STEP - 1, len(c_banks), SIDE_STEP)

        turn_unit(0, -1)
        for i, (x, g, chunk) in enumerate(c_banks):
            if chunk == 0:
                c_sb = stage.tile([P, PACK, RANGES[x] * CHUNK], F32, name="c_sb", bufs=4)
                cw = stage.tile([P, RANGES[x] * BANK], BF16, name="cw", align_bytes=64, bufs=2)
            bank = product(g, range_at[x] + chunk * CHUNK)
            weigh(g, chunk, bank, cw)
            defer(i + 1, keep_c, x, g, chunk, bank, c_sb)
            if chunk == RANGES[x] - 1:
                defer(i + 1, quantize_into, cw_q, (g, x), "cw%d%d" % (g, x), cw)
            for job, args in later[i]:
                job(*args)
            if i in unit_after:
                turn_unit(unit_after[i], i)
            if i == tol_after:
                spread_tol()
            if i in check_after:
                check = checks[check_after.index(i)]
                whole = slice(0, RANGES[check[0]] * CHUNK)
                defer(i + 1, threshold, *check, magnitude(discrepancy(*check), whole), whole)

        for job, args in later[len(c_banks)]:
            job(*args)
        for x, j in checks[len(check_after):-1]:
            whole = slice(0, RANGES[x] * CHUNK)
            threshold(x, j, magnitude(discrepancy(x, j), whole), whole)
        bank = discrepancy(*checks[-1])
        part = RANGES[-1] * CHUNK // 2
        for n in range(2):
            cols = slice(n * part, (n + 1) * part)
            threshold(*checks[-1], magnitude(bank, cols), cols)
